import numpy as np
import ml_dtypes


def mxq(x, axis, fmt="e4m3"):
    dtype, down = {"e4m3": (ml_dtypes.float8_e4m3fn, 7), "e5m2": (ml_dtypes.float8_e5m2, 14)}[fmt]
    v = np.moveaxis(np.asarray(x, np.float32).astype(ml_dtypes.bfloat16).astype(np.float64), axis, -1)
    blocks = v.reshape(v.shape[:-1] + (-1, 32))
    amax = np.abs(blocks).max(-1, keepdims=True)
    byte = np.maximum(np.where(amax > 0, np.frexp(amax)[1] - 1 + 127, 0) - down, 1)
    scale = np.exp2(byte - 127.0)
    codes = (blocks / scale).astype(np.float32).astype(dtype).astype(np.float64)
    return np.moveaxis((codes * scale).reshape(v.shape), -1, axis)


WIDE = False


def mx_kscale(k):
    if not WIDE:
        return np.ones(k)
    levels = np.array([30, -30])
    if k % 512:
        return np.exp2(np.random.permutation(np.resize(levels, k // 32))).repeat(32)
    a = np.empty((k // 512, 16))
    for p in range(k // 512):
        a[p, :8] = np.random.permutation(np.resize(levels, 8))
        for g in range(8):
            far = levels[np.abs(levels - a[p, g]) >= 10]
            a[p, g + 8] = far[np.random.randint(len(far))]
    return np.exp2(a.ravel()).repeat(32)


def f64(x):
    return np.asarray(x).astype(np.float64)


def striped(idx):
    return np.tile(np.asarray(idx).reshape(-1, 16).T, (8, 1)).astype(np.uint16)


def unstriped(offs):
    return offs[:16].T.reshape(-1).astype(np.int64)


E2M1 = np.array([0.0, 0.5, 1.0, 1.5, 2.0, 3.0, 4.0, 6.0, -0.0, -0.5, -1.0, -1.5, -2.0, -3.0, -4.0, -6.0])


def pack_weight(w, fmt):
    k, n = w.shape
    w = f64(np.asarray(w, np.float32).astype(ml_dtypes.bfloat16)).reshape(k // 32, 32, n)
    amax = np.abs(w).max(1)
    if fmt in ("e4m3", "e5m2"):
        byte = np.frexp(amax)[1] - 1 + 127 - (7 if fmt == "e4m3" else 14)
    else:
        mant, ex = np.frexp(amax / 6.0)
        byte = np.where(mant > 0.5, ex, ex - 1) + 127
    byte = np.clip(np.where(amax > 0, byte, 1), 1, 254)
    scaled = (w * np.exp2(127.0 - byte)[:, None, :]).reshape(k, n).astype(np.float32)
    by_word = np.ascontiguousarray(scaled.reshape(k // 512, 128, 4, n).transpose(0, 1, 3, 2))
    if fmt in ("e4m3", "e5m2"):
        words = by_word.astype(ml_dtypes.float8_e4m3fn if fmt == "e4m3" else ml_dtypes.float8_e5m2).view(np.uint8)
    else:
        c = by_word.astype(ml_dtypes.float4_e2m1fn).view(np.uint8) & 0xF
        words = (c[..., 0::2] | (c[..., 1::2] << 4)).reshape(k // 512, 128, 2 * n)
    return np.ascontiguousarray(words), np.ascontiguousarray(byte.astype(np.uint8).reshape(k // 512, 16, n))


def unpack_weight(words, scales, fmt):
    g, _, n = scales.shape
    words = np.ascontiguousarray(words).reshape(g, 128, n, -1)
    if fmt in ("e4m3", "e5m2"):
        vals = words.view(ml_dtypes.float8_e4m3fn if fmt == "e4m3" else ml_dtypes.float8_e5m2).astype(np.float64)
    else:
        nib = np.empty((g, 128, n, 4), np.uint8)
        nib[..., 0::2] = words & 0xF
        nib[..., 1::2] = words >> 4
        vals = E2M1[nib]
    vals = vals * np.repeat(np.exp2(scales.astype(np.float64) - 127.0), 8, axis=1)[..., None]
    return vals.transpose(0, 1, 3, 2).reshape(g * 512, n)


K, T, J, R, M, Q, O, U, X, D, N, E = 512, 1024, 256, 512, 512, 128, 64, 64, 128, 256, 256, 512


def setup_inputs():
    n = np.random.standard_normal
    idx = np.random.permutation(T)[:J]
    idx2 = np.random.permutation(J)[:O]
    idx3 = np.random.permutation(J)[:U]
    idx4 = np.random.permutation(E)[:D]
    idx5 = np.random.permutation(E)[:D]
    fk = mx_kscale(K)
    fm = mx_kscale(M)
    fr = mx_kscale(R)
    xtp = pack_weight(n((K, T)) / fk[:, None], "e4m3")
    wp = pack_weight(n((K, R)) * 1 / np.sqrt(K) * fk[:, None], "e2m1")
    xcp = pack_weight(n((M, Q)) / fm[:, None], "e4m3")
    wgp = pack_weight(n((M, R)) * 1 / np.sqrt(M) * fm[:, None] * fr, "e2m1")
    wbp = pack_weight(n((R, N)) * 1 / np.sqrt(R) / fr[:, None], "e5m2")
    return {
        "xt_words": xtp[0],
        "xt_scales": xtp[1],
        "w_words": wp[0],
        "w_scales": wp[1],
        "xc_words": xcp[0],
        "xc_scales": xcp[1],
        "wg_words": wgp[0],
        "wg_scales": wgp[1],
        "wb_words": wbp[0],
        "wb_scales": wbp[1],
        "offs": striped(idx),
        "offs2": striped(idx2),
        "offs3": striped(idx3),
        "offs4": striped(idx4),
        "offs5": striped(idx5),
    }


def reference(xt_words, xt_scales, w_words, w_scales, xc_words, xc_scales, wg_words, wg_scales, wb_words, wb_scales, offs, offs2, offs3, offs4, offs5):
    idx = unstriped(offs)
    idx2 = unstriped(offs2)
    idx3 = unstriped(offs3)
    idx4 = unstriped(offs4)
    idx5 = unstriped(offs5)
    xtu = unpack_weight(xt_words, xt_scales, "e4m3")
    wu = unpack_weight(w_words, w_scales, "e2m1")
    xcu = unpack_weight(xc_words, xc_scales, "e4m3")
    wgu = unpack_weight(wg_words, wg_scales, "e2m1")
    wbu = unpack_weight(wb_words, wb_scales, "e5m2")
    xtidxg = xtu[:, idx]
    a = wu.T @ xtidxg
    g0 = wgu.T @ xcu
    ga = g0[:, 0:1]
    gb = g0[:, 64:65]
    h1 = a[:, idx2] * ga
    h2 = a[:, idx3] * gb
    h3 = np.concatenate([h1, h2], axis=1)
    hid = np.concatenate([h3, g0], axis=1)
    hidq = mxq(hid, 0, "e4m3")
    p = wbu.T @ hidq
    pa = np.zeros((N, E))
    pa[:, idx4] = p
    pb = np.zeros((N, E))
    pb[:, idx5] = p
    y = pa + pb
    return y

@@ -1,0 +1,201 @@
+from contextlib import ExitStack
+
+import concourse.mybir as mybir
+
+K, T, J, R, M, Q, O, U, X, D, N, E = 512, 1024, 256, 512, 512, 128, 64, 64, 128, 256, 256, 512
+
+FLOPS = 2 * (K * R * J + M * R * Q + R * N * D)
+
+F32 = mybir.dt.float32
+BF16 = mybir.dt.bfloat16
+I32 = mybir.dt.int32
+U32 = mybir.dt.uint32
+U16 = mybir.dt.uint16
+U8 = mybir.dt.uint8
+E4M3 = mybir.dt.float8_e4m3fn_x4
+E5M2 = mybir.dt.float8_e5m2_x4
+E2M1 = mybir.dt.float4_e2m1fn_x4
+COPY = mybir.ActivationFunctionType.Copy
+ADD = mybir.AluOpType.add
+
+P = 128
+PACK = 4
+QUADS = 4
+LIVE = 4
+PER_COL = 16
+
+
+def tile_list_ctxthirds_solo_one_pagetwice_kernel(
+    tc, xt_words, xt_scales, w_words, w_scales, xc_words, xc_scales, wg_words, wg_scales,
+    wb_words, wb_scales, offs, offs2, offs3, offs4, offs5, out,
+):
+    nc = tc.nc
+    with ExitStack() as ctx:
+        lists = ctx.enter_context(tc.tile_pool(name="lists", bufs=1))
+        sb = ctx.enter_context(tc.tile_pool(name="sb", bufs=1))
+        ps = ctx.enter_context(tc.psum_pool(name="ps", bufs=1))
+
+        xt_plane = sb.tile([P, T], U8, align_bytes=64, tag="xt_plane")
+        nc.vector.memset(xt_plane[:].bitcast(I32), 0)
+
+        wg_raw = sb.tile([P, R // 2], I32, align_bytes=64)
+        nc.sync.dma_start(wg_raw[:], wg_words[0].bitcast(I32))
+        WG0, W0, WB0, XC0, WIDTH = 0, R, 2 * R, 2 * R + N, 2 * R + N + Q
+        staged = sb.tile([LIVE, QUADS, WIDTH // 4], I32, align_bytes=64)
+        for first, scales in ((WG0, wg_scales), (XC0, xc_scales), (W0, w_scales), (WB0, wb_scales)):
+            width = scales.shape[2]
+            nc.sync.dma_start(
+                staged[:, :, first // 4:(first + width) // 4],
+                scales[0].rearrange("(q r) c -> r q c", r=LIVE).bitcast(I32),
+            )
+        idx = lists.tile([P, J // PER_COL], U16)
+        nc.sync.dma_start(idx[:], offs)
+        xt_sb = sb.tile([P, T], I32, align_bytes=64)
+        nc.sync.dma_start(xt_sb[:], xt_words[0].rearrange("p n t -> p (n t)").bitcast(I32))
+        w_raw = sb.tile([P, R // 2], I32, align_bytes=64, tag="w_raw")
+        nc.sync.dma_start(w_raw[:], w_words[0].bitcast(I32))
+        xc_sb = sb.tile([P, Q], I32, align_bytes=64)
+        nc.sync.dma_start(xc_sb[:], xc_words[0].rearrange("p n t -> p (n t)").bitcast(I32))
+
+        xt_rows = xt_scales[0].rearrange("(q r) c -> r q c", r=LIVE)
+        for r in range(LIVE):
+            nc.sync.dma_start(xt_plane[r:P:32, :].bitcast(I32), xt_rows[r].bitcast(I32))
+        idx2 = lists.tile([P, O // PER_COL], U16)
+        nc.sync.dma_start(idx2[:], offs2)
+        idx3 = lists.tile([P, U // PER_COL], U16)
+        nc.sync.dma_start(idx3[:], offs3)
+        wb_sb = sb.tile([P, N], I32, align_bytes=64)
+        nc.sync.dma_start(wb_sb[:], wb_words[0].rearrange("p n t -> p (n t)").bitcast(I32))
+        idx4 = lists.tile([P, D // PER_COL], U16)
+        nc.sync.dma_start(idx4[:], offs4)
+        idx5 = lists.tile([P, D // PER_COL], U16)
+        nc.sync.dma_start(idx5[:], offs5)
+
+        planes = sb.tile([P, WIDTH // 4], I32, align_bytes=64)
+        nc.vector.memset(planes[:], 0)
+        pa = [sb.tile([P, E], F32, name=f"pa{n}") for n in range(N // P)]
+        pb = [sb.tile([P, E], F32, name=f"pb{n}") for n in range(N // P)]
+        for page in pa + pb:
+            nc.vector.memset(page[:], 0.0)
+
+        for q in range(1, QUADS):
+            nc.vector.tensor_copy(planes[32 * q:32 * q + LIVE, :], staged[:, q, :])
+        plane_bytes = planes[:].bitcast(U8)
+
+        def deal_words(name, raw):
+            dealt = sb.tile([P, R], U16, name=name, align_bytes=64)
+            nc.scalar.copy(
+                dealt[:].rearrange("p (t b i) -> p b t i", t=PACK, i=8),
+                raw[:].bitcast(U16).rearrange("p (b i t) -> p b t i", t=PACK, i=8),
+            )
+            return dealt
+
+        def deal_scales(name, first):
+            dealt = sb.tile([P, R], U8, name=name, align_bytes=64)
+            nc.vector.tensor_copy(
+                dealt[:].rearrange("p (t b i) -> p b t i", t=PACK, i=16),
+                plane_bytes[:, first:first + R].rearrange("p (b i t) -> p b t i", t=PACK, i=16),
+            )
+            return dealt
+
+        wg_codes = deal_words("wg_codes", wg_raw)
+        nc.scalar.copy(planes[0:LIVE, :].bitcast(U32), staged[:, 0, :].bitcast(U32))
+        wg_plane = deal_scales("wg_plane", WG0)
+        w_codes = deal_words("w_codes", w_raw)
+        w_plane = deal_scales("w_plane", W0)
+
+        xg_codes = sb.tile([P, J], U32, align_bytes=64)
+        nc.vector.tensor_copy(xg_codes[:], xt_sb[:].bitcast(U32).indirect(idx[:]))
+        xg_plane = sb.tile([P, J], U8, align_bytes=64)
+        nc.vector.tensor_copy(xg_plane[:], xt_plane[:].indirect(idx[:]))
+
+        g_ps = ps.tile([P, PACK, Q], F32)
+        for t in range(PACK):
+            cols = slice(t * P, (t + 1) * P)
+            nc.tensor.matmul_mx(
+                out=g_ps[:, t, :], lhsT=wg_codes[:, cols].bitcast(E2M1), lhsT_scale=wg_plane[:, cols],
+                rhs=xc_sb[:].bitcast(E4M3), rhs_scale=plane_bytes[:, XC0:XC0 + Q], start=True, stop=True,
+            )
+        hid_g = sb.tile([P, Q, PACK], BF16, align_bytes=64, tag="w_raw")
+        nc.scalar.copy(hid_g[:], g_ps[:].rearrange("p t q -> p q t"))
+        gains = sb.tile([P, PACK, 2], F32)
+        nc.scalar.copy(gains[:], g_ps[:, :, 0:Q:O])
+        g_codes = sb.tile([P, Q], U32, align_bytes=64)
+        g_plane = sb.tile([P, Q], U8, align_bytes=64, tag="xt_plane")
+        nc.vector.quantize_mx(
+            out=g_codes[:].bitcast(E4M3), scales=g_plane[:], in_=hid_g[:].rearrange("p q t -> p (q t)"))
+
+        h = sb.tile([P, 2, PACK, O], F32)
+        a_sb = []
+        for t in range(PACK):
+            cols = slice(t * P, (t + 1) * P)
+            a_ps = ps.tile([P, J], F32, name=f"a_ps{t}")
+            nc.tensor.matmul_mx(
+                out=a_ps[:], lhsT=w_codes[:, cols].bitcast(E2M1), lhsT_scale=w_plane[:, cols],
+                rhs=xg_codes[:].bitcast(E4M3), rhs_scale=xg_plane[:], start=True, stop=True,
+            )
+            a_t = sb.tile([P, J], F32, name=f"a{t}")
+            nc.vector.tensor_copy(a_t[:], a_ps[:])
+            a_sb.append(a_t)
+        for t, s in ((0, 0), (0, 1), (1, 0), (1, 1), (2, 0), (3, 0), (2, 1), (3, 1)):
+            nc.scalar.activation(
+                h[:, s, t, :], a_sb[t][:].indirect((idx2, idx3)[s][:]), COPY, scale=gains[:, t, s:s + 1])
+
+        def out_product(bank, n, codes, plane):
+            cols = slice(n * P, (n + 1) * P)
+            nc.tensor.matmul_mx(
+                out=bank, lhsT=wb_sb[:, cols].bitcast(E5M2),
+                lhsT_scale=plane_bytes[:, WB0 + n * P:WB0 + (n + 1) * P],
+                rhs=codes[:].bitcast(E4M3), rhs_scale=plane[:], start=True, stop=True,
+            )
+
+        def put(engine, page, places, first, values):
+            count = values.shape[1]
+            window = page[:].indirect(places[:, first // PER_COL:(first + count) // PER_COL])
+            if engine == "vector":
+                nc.vector.tensor_copy(window, values)
+            else:
+                nc.scalar.activation(window, values, COPY)
+
+        pg_ps = ps.tile([P, N // P, Q], F32)
+        for n in range(N // P):
+            out_product(pg_ps[:, n, :], n, g_codes, g_plane)
+        p_g = sb.tile([P, N // P, Q], F32)
+        nc.vector.tensor_copy(p_g[:], pg_ps[:])
+        put("vector", pa[0], idx4, X, p_g[:, 0, :])
+
+        hid_h = sb.tile([P, X, PACK], BF16, align_bytes=64)
+        h_codes = sb.tile([P, X], U32, align_bytes=64)
+        h_plane = sb.tile([P, X], U8, align_bytes=64)
+        for s in range(2):
+            nc.vector.tensor_copy(
+                hid_h[:, s * O:(s + 1) * O, :].rearrange("p (c i) t -> p c t i", i=4),
+                h[:, s].rearrange("p t (c i) -> p c t i", i=4))
+        nc.vector.quantize_mx(
+            out=h_codes[:].bitcast(E4M3), scales=h_plane[:], in_=hid_h[:].rearrange("p x t -> p (x t)"))
+
+        put("scalar", pb[0], idx5, X, p_g[:, 0, :])
+        put("scalar", pb[1], idx5, X, p_g[:, 1, :])
+        put("vector", pa[1], idx4, X, p_g[:, 1, 0:O])
+
+        p_h = []
+        for n in range(N // P):
+            ph_ps = ps.tile([P, X], F32, name=f"ph_ps{n}")
+            out_product(ph_ps[:], n, h_codes, h_plane)
+            p_hn = sb.tile([P, X], F32, name=f"p_h{n}")
+            nc.vector.tensor_copy(p_hn[:], ph_ps[:])
+            p_h.append(p_hn)
+
+        put("vector", pa[0], idx4, 0, p_h[0][:])
+        put("scalar", pb[0], idx5, 0, p_h[0][:])
+        y0 = sb.tile([P, E], F32)
+        nc.vector.tensor_tensor(y0[:], pa[0][:], pb[0][:], ADD)
+        nc.sync.dma_start(out[0:P, :], y0[:])
+        put("scalar", pa[1], idx4, X + O, p_g[:, 1, O:Q])
+        put("scalar", pb[1], idx5, 0, p_h[1][:])
+        put("vector", pa[1], idx4, 0, p_h[1][:])
+        for half, queue in enumerate((nc.sync, nc.scalar)):
+            cols = slice(half * E // 2, (half + 1) * E // 2)
+            y1 = sb.tile([P, E // 2], F32, name=f"y1_{half}")
+            nc.vector.tensor_tensor(y1[:], pa[1][:, cols], pb[1][:, cols], ADD)
+            queue.dma_start(out[P:2 * P, cols], y1[:])

@@ -38,34 +38,36 @@ def tile_list_ctxthirds_solo_one_pagetwice_kernel(
         xt_plane = sb.tile([P, T], U8, align_bytes=64, tag="xt_plane")
         nc.vector.memset(xt_plane[:].bitcast(I32), 0)
 
-        wg_raw = sb.tile([P, R // 2], I32, align_bytes=64)
-        nc.sync.dma_start(wg_raw[:], wg_words[0].bitcast(I32))
-        WG0, W0, WB0, XC0, WIDTH = 0, R, 2 * R, 2 * R + N, 2 * R + N + Q
+        idx = lists.tile([P, J // PER_COL], U16)
+        nc.sync.dma_start(idx[:], offs)
+        WG0, W0, XC0, WIDTH = 0, R, 2 * R, 2 * R + Q
         staged = sb.tile([LIVE, QUADS, WIDTH // 4], I32, align_bytes=64)
-        for first, scales in ((WG0, wg_scales), (XC0, xc_scales), (W0, w_scales), (WB0, wb_scales)):
+        for first, scales in ((WG0, wg_scales), (XC0, xc_scales), (W0, w_scales)):
             width = scales.shape[2]
             nc.sync.dma_start(
                 staged[:, :, first // 4:(first + width) // 4],
                 scales[0].rearrange("(q r) c -> r q c", r=LIVE).bitcast(I32),
             )
-        idx = lists.tile([P, J // PER_COL], U16)
-        nc.sync.dma_start(idx[:], offs)
+        wg_raw = sb.tile([P, R // 2], I32, align_bytes=64)
+        nc.sync.dma_start(wg_raw[:], wg_words[0].bitcast(I32))
+        xc_sb = sb.tile([P, Q], I32, align_bytes=64)
+        nc.sync.dma_start(xc_sb[:], xc_words[0].rearrange("p n t -> p (n t)").bitcast(I32))
         xt_sb = sb.tile([P, T], I32, align_bytes=64)
         nc.sync.dma_start(xt_sb[:], xt_words[0].rearrange("p n t -> p (n t)").bitcast(I32))
         w_raw = sb.tile([P, R // 2], I32, align_bytes=64, tag="w_raw")
         nc.sync.dma_start(w_raw[:], w_words[0].bitcast(I32))
-        xc_sb = sb.tile([P, Q], I32, align_bytes=64)
-        nc.sync.dma_start(xc_sb[:], xc_words[0].rearrange("p n t -> p (n t)").bitcast(I32))
 
         xt_rows = xt_scales[0].rearrange("(q r) c -> r q c", r=LIVE)
         for r in range(LIVE):
             nc.sync.dma_start(xt_plane[r:P:32, :].bitcast(I32), xt_rows[r].bitcast(I32))
+        wb_staged = sb.tile([LIVE, QUADS, N // 4], I32, align_bytes=64)
+        nc.sync.dma_start(wb_staged[:], wb_scales[0].rearrange("(q r) c -> r q c", r=LIVE).bitcast(I32))
+        wb_sb = sb.tile([P, N], I32, align_bytes=64)
+        nc.sync.dma_start(wb_sb[:], wb_words[0].rearrange("p n t -> p (n t)").bitcast(I32))
         idx2 = lists.tile([P, O // PER_COL], U16)
         nc.sync.dma_start(idx2[:], offs2)
         idx3 = lists.tile([P, U // PER_COL], U16)
         nc.sync.dma_start(idx3[:], offs3)
-        wb_sb = sb.tile([P, N], I32, align_bytes=64)
-        nc.sync.dma_start(wb_sb[:], wb_words[0].rearrange("p n t -> p (n t)").bitcast(I32))
         idx4 = lists.tile([P, D // PER_COL], U16)
         nc.sync.dma_start(idx4[:], offs4)
         idx5 = lists.tile([P, D // PER_COL], U16)
@@ -73,12 +75,16 @@ def tile_list_ctxthirds_solo_one_pagetwice_kernel(
 
         planes = sb.tile([P, WIDTH // 4], I32, align_bytes=64)
         nc.vector.memset(planes[:], 0)
+        wb_plane = sb.tile([P, N // 4], I32, align_bytes=64)
+        nc.vector.memset(wb_plane[:], 0)
         pa = [sb.tile([P, E], F32, name=f"pa{n}") for n in range(N // P)]
         pb = [sb.tile([P, E], F32, name=f"pb{n}") for n in range(N // P)]
-        for page in pa + pb:
-            nc.vector.memset(page[:], 0.0)
+        for page in pa:
+            nc.vector.memset(page[:].bitcast(I32), 0)
+        for page in pb:
+            nc.gpsimd.memset(page[:], 0.0)
 
-        for q in range(1, QUADS):
+        for q in range(QUADS):
             nc.vector.tensor_copy(planes[32 * q:32 * q + LIVE, :], staged[:, q, :])
         plane_bytes = planes[:].bitcast(U8)
 
@@ -99,7 +105,6 @@ def tile_list_ctxthirds_solo_one_pagetwice_kernel(
             return dealt
 
         wg_codes = deal_words("wg_codes", wg_raw)
-        nc.scalar.copy(planes[0:LIVE, :].bitcast(U32), staged[:, 0, :].bitcast(U32))
         wg_plane = deal_scales("wg_plane", WG0)
         w_codes = deal_words("w_codes", w_raw)
         w_plane = deal_scales("w_plane", W0)
@@ -108,6 +113,9 @@ def tile_list_ctxthirds_solo_one_pagetwice_kernel(
         nc.vector.tensor_copy(xg_codes[:], xt_sb[:].bitcast(U32).indirect(idx[:]))
         xg_plane = sb.tile([P, J], U8, align_bytes=64)
         nc.vector.tensor_copy(xg_plane[:], xt_plane[:].indirect(idx[:]))
+
+        for q in range(QUADS):
+            nc.vector.tensor_copy(wb_plane[32 * q:32 * q + LIVE, :], wb_staged[:, q, :])
 
         g_ps = ps.tile([P, PACK, Q], F32)
         for t in range(PACK):
@@ -125,17 +133,20 @@ def tile_list_ctxthirds_solo_one_pagetwice_kernel(
         nc.vector.quantize_mx(
             out=g_codes[:].bitcast(E4M3), scales=g_plane[:], in_=hid_g[:].rearrange("p q t -> p (q t)"))
 
-        h = sb.tile([P, 2, PACK, O], F32)
+        h = sb.tile([P, 2, PACK, O], F32, tag="h")
         a_sb = []
         for t in range(PACK):
             cols = slice(t * P, (t + 1) * P)
-            a_ps = ps.tile([P, J], F32, name=f"a_ps{t}")
+            a_ps = ps.tile([P, J], F32, name=f"a_ps{t}", tag=f"a_ps{t}")
             nc.tensor.matmul_mx(
                 out=a_ps[:], lhsT=w_codes[:, cols].bitcast(E2M1), lhsT_scale=w_plane[:, cols],
                 rhs=xg_codes[:].bitcast(E4M3), rhs_scale=xg_plane[:], start=True, stop=True,
             )
             a_t = sb.tile([P, J], F32, name=f"a{t}")
-            nc.vector.tensor_copy(a_t[:], a_ps[:])
+            if t == 0:
+                nc.scalar.copy(a_t[:], a_ps[:])
+            else:
+                nc.vector.tensor_copy(a_t[:], a_ps[:])
             a_sb.append(a_t)
         for t, s in ((0, 0), (0, 1), (1, 0), (1, 1), (2, 0), (3, 0), (2, 1), (3, 1)):
             nc.scalar.activation(
@@ -145,7 +156,7 @@ def tile_list_ctxthirds_solo_one_pagetwice_kernel(
             cols = slice(n * P, (n + 1) * P)
             nc.tensor.matmul_mx(
                 out=bank, lhsT=wb_sb[:, cols].bitcast(E5M2),
-                lhsT_scale=plane_bytes[:, WB0 + n * P:WB0 + (n + 1) * P],
+                lhsT_scale=wb_plane[:].bitcast(U8)[:, cols],
                 rhs=codes[:].bitcast(E4M3), rhs_scale=plane[:], start=True, stop=True,
             )
 
@@ -157,12 +168,14 @@ def tile_list_ctxthirds_solo_one_pagetwice_kernel(
             else:
                 nc.scalar.activation(window, values, COPY)
 
-        pg_ps = ps.tile([P, N // P, Q], F32)
+        pg_ps = []
         for n in range(N // P):
-            out_product(pg_ps[:, n, :], n, g_codes, g_plane)
-        p_g = sb.tile([P, N // P, Q], F32)
-        nc.vector.tensor_copy(p_g[:], pg_ps[:])
-        put("vector", pa[0], idx4, X, p_g[:, 0, :])
+            bank = ps.tile([P, Q], F32, name=f"pg_ps{n}", tag=f"a_ps{n}")
+            out_product(bank[:], n, g_codes, g_plane)
+            pg_ps.append(bank)
+        p_g0 = sb.tile([P, Q], F32)
+        nc.vector.tensor_copy(p_g0[:], pg_ps[0][:])
+        put("vector", pa[0], idx4, X, p_g0[:])
 
         hid_h = sb.tile([P, X, PACK], BF16, align_bytes=64)
         h_codes = sb.tile([P, X], U32, align_bytes=64)
@@ -174,26 +187,26 @@ def tile_list_ctxthirds_solo_one_pagetwice_kernel(
         nc.vector.quantize_mx(
             out=h_codes[:].bitcast(E4M3), scales=h_plane[:], in_=hid_h[:].rearrange("p x t -> p (x t)"))
 
-        put("scalar", pb[0], idx5, X, p_g[:, 0, :])
-        put("scalar", pb[1], idx5, X, p_g[:, 1, :])
-        put("vector", pa[1], idx4, X, p_g[:, 1, 0:O])
+        put("scalar", pb[0], idx5, X, p_g0[:])
+        p_g1 = sb.tile([P, Q], F32, tag="h")
+        nc.vector.tensor_copy(p_g1[:], pg_ps[1][:])
+        put("vector", pa[1], idx4, X, p_g1[:, 0:O])
+        put("scalar", pb[1], idx5, X, p_g1[:])
 
-        p_h = []
+        ph_ps = ps.tile([P, N // P, X], F32)
         for n in range(N // P):
-            ph_ps = ps.tile([P, X], F32, name=f"ph_ps{n}")
-            out_product(ph_ps[:], n, h_codes, h_plane)
-            p_hn = sb.tile([P, X], F32, name=f"p_h{n}")
-            nc.vector.tensor_copy(p_hn[:], ph_ps[:])
-            p_h.append(p_hn)
+            out_product(ph_ps[:, n, :], n, h_codes, h_plane)
+        p_h = sb.tile([P, N // P, X], F32)
+        nc.vector.tensor_copy(p_h[:], ph_ps[:])
 
-        put("vector", pa[0], idx4, 0, p_h[0][:])
-        put("scalar", pb[0], idx5, 0, p_h[0][:])
+        put("vector", pa[0], idx4, 0, p_h[:, 0, :])
+        put("scalar", pb[0], idx5, 0, p_h[:, 0, :])
         y0 = sb.tile([P, E], F32)
         nc.vector.tensor_tensor(y0[:], pa[0][:], pb[0][:], ADD)
         nc.sync.dma_start(out[0:P, :], y0[:])
-        put("scalar", pa[1], idx4, X + O, p_g[:, 1, O:Q])
-        put("scalar", pb[1], idx5, 0, p_h[1][:])
-        put("vector", pa[1], idx4, 0, p_h[1][:])
+        put("scalar", pa[1], idx4, X + O, p_g1[:, O:Q])
+        put("scalar", pb[1], idx5, 0, p_h[:, 1, :])
+        put("vector", pa[1], idx4, 0, p_h[:, 1, :])
         for half, queue in enumerate((nc.sync, nc.scalar)):
             cols = slice(half * E // 2, (half + 1) * E // 2)
             y1 = sb.tile([P, E // 2], F32, name=f"y1_{half}")

from contextlib import ExitStack

import concourse.mybir as mybir

K, T, J, R, M, Q, O, U, X, D, N, E = 512, 1024, 256, 512, 512, 128, 64, 64, 128, 256, 256, 512

FLOPS = 2 * (K * R * J + M * R * Q + R * N * D)

F32 = mybir.dt.float32
BF16 = mybir.dt.bfloat16
I32 = mybir.dt.int32
U32 = mybir.dt.uint32
U16 = mybir.dt.uint16
U8 = mybir.dt.uint8
E4M3 = mybir.dt.float8_e4m3fn_x4
E5M2 = mybir.dt.float8_e5m2_x4
E2M1 = mybir.dt.float4_e2m1fn_x4
COPY = mybir.ActivationFunctionType.Copy
ADD = mybir.AluOpType.add

P = 128
PACK = 4
QUADS = 4
LIVE = 4
PER_COL = 16


def tile_list_ctxthirds_solo_one_pagetwice_kernel(
    tc, xt_words, xt_scales, w_words, w_scales, xc_words, xc_scales, wg_words, wg_scales,
    wb_words, wb_scales, offs, offs2, offs3, offs4, offs5, out,
):
    nc = tc.nc
    with ExitStack() as ctx:
        lists = ctx.enter_context(tc.tile_pool(name="lists", bufs=1))
        sb = ctx.enter_context(tc.tile_pool(name="sb", bufs=1))
        ps = ctx.enter_context(tc.psum_pool(name="ps", bufs=1))

        xt_plane = sb.tile([P, T], U8, align_bytes=64, tag="xt_plane")
        nc.vector.memset(xt_plane[:].bitcast(I32), 0)

        idx = lists.tile([P, J // PER_COL], U16)
        nc.sync.dma_start(idx[:], offs)
        WG0, W0, XC0, WIDTH = 0, R, 2 * R, 2 * R + Q
        staged = sb.tile([LIVE, QUADS, WIDTH // 4], I32, align_bytes=64)
        for first, scales in ((WG0, wg_scales), (XC0, xc_scales), (W0, w_scales)):
            width = scales.shape[2]
            nc.sync.dma_start(
                staged[:, :, first // 4:(first + width) // 4],
                scales[0].rearrange("(q r) c -> r q c", r=LIVE).bitcast(I32),
            )
        wg_raw = sb.tile([P, R // 2], I32, align_bytes=64)
        nc.sync.dma_start(wg_raw[:], wg_words[0].bitcast(I32))
        xc_sb = sb.tile([P, Q], I32, align_bytes=64)
        nc.sync.dma_start(xc_sb[:], xc_words[0].rearrange("p n t -> p (n t)").bitcast(I32))
        xt_sb = sb.tile([P, T], I32, align_bytes=64)
        nc.sync.dma_start(xt_sb[:], xt_words[0].rearrange("p n t -> p (n t)").bitcast(I32))
        w_raw = sb.tile([P, R // 2], I32, align_bytes=64, tag="w_raw")
        nc.sync.dma_start(w_raw[:], w_words[0].bitcast(I32))

        xt_rows = xt_scales[0].rearrange("(q r) c -> r q c", r=LIVE)
        for r in range(LIVE):
            nc.sync.dma_start(xt_plane[r:P:32, :].bitcast(I32), xt_rows[r].bitcast(I32))
        wb_staged = sb.tile([LIVE, QUADS, N // 4], I32, align_bytes=64)
        nc.sync.dma_start(wb_staged[:], wb_scales[0].rearrange("(q r) c -> r q c", r=LIVE).bitcast(I32))
        wb_sb = sb.tile([P, N], I32, align_bytes=64)
        nc.sync.dma_start(wb_sb[:], wb_words[0].rearrange("p n t -> p (n t)").bitcast(I32))
        idx2 = lists.tile([P, O // PER_COL], U16)
        nc.sync.dma_start(idx2[:], offs2)
        idx3 = lists.tile([P, U // PER_COL], U16)
        nc.sync.dma_start(idx3[:], offs3)
        idx4 = lists.tile([P, D // PER_COL], U16)
        nc.sync.dma_start(idx4[:], offs4)
        idx5 = lists.tile([P, D // PER_COL], U16)
        nc.sync.dma_start(idx5[:], offs5)

        planes = sb.tile([P, WIDTH // 4], I32, align_bytes=64)
        nc.vector.memset(planes[:], 0)
        wb_plane = sb.tile([P, N // 4], I32, align_bytes=64)
        nc.vector.memset(wb_plane[:], 0)
        pa = [sb.tile([P, E], F32, name=f"pa{n}") for n in range(N // P)]
        pb = [sb.tile([P, E], F32, name=f"pb{n}") for n in range(N // P)]
        for page in pa:
            nc.vector.memset(page[:].bitcast(I32), 0)
        for page in pb:
            nc.gpsimd.memset(page[:], 0.0)

        for q in range(QUADS):
            nc.vector.tensor_copy(planes[32 * q:32 * q + LIVE, :], staged[:, q, :])
        plane_bytes = planes[:].bitcast(U8)

        def deal_words(name, raw):
            dealt = sb.tile([P, R], U16, name=name, align_bytes=64)
            nc.scalar.copy(
                dealt[:].rearrange("p (t b i) -> p b t i", t=PACK, i=8),
                raw[:].bitcast(U16).rearrange("p (b i t) -> p b t i", t=PACK, i=8),
            )
            return dealt

        def deal_scales(name, first):
            dealt = sb.tile([P, R], U8, name=name, align_bytes=64)
            nc.vector.tensor_copy(
                dealt[:].rearrange("p (t b i) -> p b t i", t=PACK, i=16),
                plane_bytes[:, first:first + R].rearrange("p (b i t) -> p b t i", t=PACK, i=16),
            )
            return dealt

        wg_codes = deal_words("wg_codes", wg_raw)
        wg_plane = deal_scales("wg_plane", WG0)
        w_codes = deal_words("w_codes", w_raw)
        w_plane = deal_scales("w_plane", W0)

        xg_codes = sb.tile([P, J], U32, align_bytes=64)
        nc.vector.tensor_copy(xg_codes[:], xt_sb[:].bitcast(U32).indirect(idx[:]))
        xg_plane = sb.tile([P, J], U8, align_bytes=64)
        nc.vector.tensor_copy(xg_plane[:], xt_plane[:].indirect(idx[:]))

        for q in range(QUADS):
            nc.vector.tensor_copy(wb_plane[32 * q:32 * q + LIVE, :], wb_staged[:, q, :])

        g_ps = ps.tile([P, PACK, Q], F32)
        for t in range(PACK):
            cols = slice(t * P, (t + 1) * P)
            nc.tensor.matmul_mx(
                out=g_ps[:, t, :], lhsT=wg_codes[:, cols].bitcast(E2M1), lhsT_scale=wg_plane[:, cols],
                rhs=xc_sb[:].bitcast(E4M3), rhs_scale=plane_bytes[:, XC0:XC0 + Q], start=True, stop=True,
            )
        hid_g = sb.tile([P, Q, PACK], BF16, align_bytes=64, tag="w_raw")
        nc.scalar.copy(hid_g[:], g_ps[:].rearrange("p t q -> p q t"))
        gains = sb.tile([P, PACK, 2], F32)
        nc.scalar.copy(gains[:], g_ps[:, :, 0:Q:O])
        g_codes = sb.tile([P, Q], U32, align_bytes=64)
        g_plane = sb.tile([P, Q], U8, align_bytes=64, tag="xt_plane")
        nc.vector.quantize_mx(
            out=g_codes[:].bitcast(E4M3), scales=g_plane[:], in_=hid_g[:].rearrange("p q t -> p (q t)"))

        h = sb.tile([P, 2, PACK, O], F32, tag="h")
        a_sb = []
        for t in range(PACK):
            cols = slice(t * P, (t + 1) * P)
            a_ps = ps.tile([P, J], F32, name=f"a_ps{t}", tag=f"a_ps{t}")
            nc.tensor.matmul_mx(
                out=a_ps[:], lhsT=w_codes[:, cols].bitcast(E2M1), lhsT_scale=w_plane[:, cols],
                rhs=xg_codes[:].bitcast(E4M3), rhs_scale=xg_plane[:], start=True, stop=True,
            )
            a_t = sb.tile([P, J], F32, name=f"a{t}")
            if t == 0:
                nc.scalar.copy(a_t[:], a_ps[:])
            else:
                nc.vector.tensor_copy(a_t[:], a_ps[:])
            a_sb.append(a_t)
        for t, s in ((0, 0), (0, 1), (1, 0), (1, 1), (2, 0), (3, 0), (2, 1), (3, 1)):
            nc.scalar.activation(
                h[:, s, t, :], a_sb[t][:].indirect((idx2, idx3)[s][:]), COPY, scale=gains[:, t, s:s + 1])

        def out_product(bank, n, codes, plane):
            cols = slice(n * P, (n + 1) * P)
            nc.tensor.matmul_mx(
                out=bank, lhsT=wb_sb[:, cols].bitcast(E5M2),
                lhsT_scale=wb_plane[:].bitcast(U8)[:, cols],
                rhs=codes[:].bitcast(E4M3), rhs_scale=plane[:], start=True, stop=True,
            )

        def put(engine, page, places, first, values):
            count = values.shape[1]
            window = page[:].indirect(places[:, first // PER_COL:(first + count) // PER_COL])
            if engine == "vector":
                nc.vector.tensor_copy(window, values)
            else:
                nc.scalar.activation(window, values, COPY)

        pg_ps = []
        for n in range(N // P):
            bank = ps.tile([P, Q], F32, name=f"pg_ps{n}", tag=f"a_ps{n}")
            out_product(bank[:], n, g_codes, g_plane)
            pg_ps.append(bank)
        p_g0 = sb.tile([P, Q], F32)
        nc.vector.tensor_copy(p_g0[:], pg_ps[0][:])
        put("vector", pa[0], idx4, X, p_g0[:])

        hid_h = sb.tile([P, X, PACK], BF16, align_bytes=64)
        h_codes = sb.tile([P, X], U32, align_bytes=64)
        h_plane = sb.tile([P, X], U8, align_bytes=64)
        for s in range(2):
            nc.vector.tensor_copy(
                hid_h[:, s * O:(s + 1) * O, :].rearrange("p (c i) t -> p c t i", i=4),
                h[:, s].rearrange("p t (c i) -> p c t i", i=4))
        nc.vector.quantize_mx(
            out=h_codes[:].bitcast(E4M3), scales=h_plane[:], in_=hid_h[:].rearrange("p x t -> p (x t)"))

        put("scalar", pb[0], idx5, X, p_g0[:])
        p_g1 = sb.tile([P, Q], F32, tag="h")
        nc.vector.tensor_copy(p_g1[:], pg_ps[1][:])
        put("vector", pa[1], idx4, X, p_g1[:, 0:O])
        put("scalar", pb[1], idx5, X, p_g1[:])

        ph_ps = ps.tile([P, N // P, X], F32)
        for n in range(N // P):
            out_product(ph_ps[:, n, :], n, h_codes, h_plane)
        p_h = sb.tile([P, N // P, X], F32)
        nc.vector.tensor_copy(p_h[:], ph_ps[:])

        put("vector", pa[0], idx4, 0, p_h[:, 0, :])
        put("scalar", pb[0], idx5, 0, p_h[:, 0, :])
        y0 = sb.tile([P, E], F32)
        nc.vector.tensor_tensor(y0[:], pa[0][:], pb[0][:], ADD)
        nc.sync.dma_start(out[0:P, :], y0[:])
        put("scalar", pa[1], idx4, X + O, p_g1[:, O:Q])
        put("scalar", pb[1], idx5, 0, p_h[:, 1, :])
        put("vector", pa[1], idx4, 0, p_h[:, 1, :])
        for half, queue in enumerate((nc.sync, nc.scalar)):
            cols = slice(half * E // 2, (half + 1) * E // 2)
            y1 = sb.tile([P, E // 2], F32, name=f"y1_{half}")
            nc.vector.tensor_tensor(y1[:], pa[1][:, cols], pb[1][:, cols], ADD)
            queue.dma_start(out[P:2 * P, cols], y1[:])
